import numpy as np
import ml_dtypes


def mxq(x, axis, fmt="e4m3"):
    dtype, down = {"e4m3": (ml_dtypes.float8_e4m3fn, 7), "e5m2": (ml_dtypes.float8_e5m2, 14)}[fmt]
    v = np.moveaxis(np.asarray(x, np.float32).astype(ml_dtypes.bfloat16).astype(np.float64), axis, -1)
    blocks = v.reshape(v.shape[:-1] + (-1, 32))
    amax = np.abs(blocks).max(-1, keepdims=True)
    byte = np.maximum(np.where(amax > 0, np.frexp(amax)[1] - 1 + 127, 0) - down, 1)
    scale = np.exp2(byte - 127.0)
    codes = (blocks / scale).astype(np.float32).astype(dtype).astype(np.float64)
    return np.moveaxis((codes * scale).reshape(v.shape), -1, axis)


WIDE = False


def mx_kscale(k):
    if not WIDE:
        return np.ones(k)
    levels = np.array([10, -10, 5, -5, 0])
    if k % 512:
        return np.exp2(np.random.permutation(np.resize(levels, k // 32))).repeat(32)
    a = np.empty((k // 512, 16))
    for p in range(k // 512):
        a[p, :8] = np.random.permutation(np.resize(levels, 8))
        for g in range(8):
            far = levels[np.abs(levels - a[p, g]) >= 10]
            a[p, g + 8] = far[np.random.randint(len(far))]
    return np.exp2(a.ravel()).repeat(32)


def f64(x):
    return np.asarray(x).astype(np.float64)


def striped(idx):
    return np.tile(np.asarray(idx).reshape(-1, 16).T, (8, 1)).astype(np.uint16)


def unstriped(offs):
    return offs[:16].T.reshape(-1).astype(np.int64)


def striped8(idx):
    return np.asarray(idx).reshape(8, -1, 16).transpose(0, 2, 1).reshape(128, -1).astype(np.uint16)


def unstriped8(offs):
    return offs.reshape(8, 16, -1).transpose(0, 2, 1).reshape(8, -1).astype(np.int64)


def pick8(x, idx, run):
    r = np.arange(len(x))
    return x[r[:, None], idx[r % (8 * run) // run]]


E2M1 = np.array([0.0, 0.5, 1.0, 1.5, 2.0, 3.0, 4.0, 6.0, -0.0, -0.5, -1.0, -1.5, -2.0, -3.0, -4.0, -6.0])


def pack_weight(w, fmt):
    k, n = w.shape
    w = f64(np.asarray(w, np.float32).astype(ml_dtypes.bfloat16)).reshape(k // 32, 32, n)
    amax = np.abs(w).max(1)
    if fmt == "e4m3":
        byte = np.frexp(amax)[1] - 1 + 127 - 7
    else:
        mant, ex = np.frexp(amax / 6.0)
        byte = np.where(mant > 0.5, ex, ex - 1) + 127
    byte = np.clip(np.where(amax > 0, byte, 1), 1, 254)
    scaled = (w * np.exp2(127.0 - byte)[:, None, :]).reshape(k, n).astype(np.float32)
    by_word = np.ascontiguousarray(scaled.reshape(k // 512, 128, 4, n).transpose(0, 1, 3, 2))
    if fmt == "e4m3":
        words = by_word.astype(ml_dtypes.float8_e4m3fn).view(np.uint8)
    else:
        c = by_word.astype(ml_dtypes.float4_e2m1fn).view(np.uint8) & 0xF
        words = (c[..., 0::2] | (c[..., 1::2] << 4)).reshape(k // 512, 128, 2 * n)
    return np.ascontiguousarray(words), np.ascontiguousarray(byte.astype(np.uint8).reshape(k // 512, 16, n))


def unpack_weight(words, scales, fmt):
    g, _, n = scales.shape
    words = np.ascontiguousarray(words).reshape(g, 128, n, -1)
    if fmt == "e4m3":
        vals = words.view(ml_dtypes.float8_e4m3fn).astype(np.float64)
    else:
        nib = np.empty((g, 128, n, 4), np.uint8)
        nib[..., 0::2] = words & 0xF
        nib[..., 1::2] = words >> 4
        vals = E2M1[nib]
    vals = vals * np.repeat(np.exp2(scales.astype(np.float64) - 127.0), 8, axis=1)[..., None]
    return vals.transpose(0, 1, 3, 2).reshape(g * 512, n)


K, J, R, T, F, C, O, N, S, Z = 512, 256, 512, 512, 2048, 512, 128, 256, 512, 512


def setup_inputs():
    n = np.random.standard_normal
    idx = np.random.permutation(T)[:J]
    idx2 = np.stack([np.random.permutation(F)[:R] for _ in range(8)])
    idx3 = np.random.permutation(C)[:J]
    idx4 = np.random.permutation(C)[:O]
    idx5 = np.stack([np.random.permutation(C)[:O] for _ in range(8)])
    idx6 = np.random.permutation(S)[:N]
    idx7 = np.stack([np.random.permutation(Z)[:N] for _ in range(8)])
    fk = mx_kscale(K)
    fr = mx_kscale(R)
    xtp = pack_weight(n((K, T)) * fk[:, None], "e4m3")
    return {
        "xt_words": xtp[0],
        "xt_scales": xtp[1],
        "ua": (np.random.randint(-7, 8, (K, F)).astype(np.float64)).astype(np.float32),
        "ha": ((np.random.randint(8, 25, (K, 1)) / 1024.0) / fk[:, None]).astype(np.float32),
        "sa": (np.random.uniform(0.5, 1.6, (R, 1)) * fr[:, None]).astype(np.float32),
        "sb": (np.random.uniform(0.5, 1.6, (R, 1)) * fr[:, None]).astype(np.float32),
        "va": (np.random.randint(-7, 8, (R, S)).astype(np.float64)).astype(np.float32),
        "vb": (np.random.randint(-7, 8, (R, Z)).astype(np.float64)).astype(np.float32),
        "ea": ((np.random.randint(10, 25, (R, 1)) / 1024.0) / fr[:, None]).astype(np.float32),
        "eb": ((np.random.randint(4, 13, (R, 1)) / 1024.0) / fr[:, None]).astype(np.float32),
        "offs": striped(idx),
        "offs2": striped8(idx2),
        "offs3": striped(idx3),
        "offs4": striped(idx4),
        "offs5": striped8(idx5),
        "offs6": striped(idx6),
        "offs7": striped8(idx7),
    }


def reference(xt_words, xt_scales, ua, ha, sa, sb, va, vb, ea, eb, offs, offs2, offs3, offs4, offs5, offs6, offs7):
    idx = unstriped(offs)
    idx2 = unstriped8(offs2)
    idx3 = unstriped(offs3)
    idx4 = unstriped(offs4)
    idx5 = unstriped8(offs5)
    idx6 = unstriped(offs6)
    idx7 = unstriped8(offs7)
    xtu = unpack_weight(xt_words, xt_scales, "e4m3")
    wc = pick8(f64(ua), idx2, 64) * f64(ha)
    wcq = mxq(wc, 0, "e4m3")
    xtidxg = xtu[:, idx]
    a = wcq.T @ xtidxg
    pw = np.zeros((R, C))
    pw[:, idx3] = a
    hid = np.abs(pw[:, idx4] * f64(sa) - pick8(pw, idx5, 64) * f64(sb))
    vc = f64(va)[:, idx6] * f64(ea) + pick8(f64(vb), idx7, 64) * f64(eb)
    vcq = mxq(vc, 0, "e4m3")
    hidq = mxq(hid, 0, "e4m3")
    y = vcq.T @ hidq
    return y

@@ -1,0 +1,208 @@
+from contextlib import ExitStack
+
+import concourse.mybir as mybir
+
+K, J, R, T, F, C, O, N, S, Z = 512, 256, 512, 512, 2048, 512, 128, 256, 512, 512
+FLOPS = 2 * K * R * J + 2 * R * N * O
+
+F32 = mybir.dt.float32
+BF16 = mybir.dt.bfloat16
+I32 = mybir.dt.int32
+U32 = mybir.dt.uint32
+U16 = mybir.dt.uint16
+U8 = mybir.dt.uint8
+FP8X4 = mybir.dt.float8_e4m3fn_x4
+ALU = mybir.AluOpType
+ACT = mybir.ActivationFunctionType
+
+P = 128
+PACK = 4
+
+
+def tile_picked_tokens_codes_one_boardmixed_basedetail_plain_kernel(
+    tc, xt_words, xt_scales, ua, ha, sa, sb, va, vb, ea, eb, offs, offs2, offs3, offs4, offs5, offs6, offs7, out
+):
+    nc = tc.nc
+    with ExitStack() as ctx:
+        lists = ctx.enter_context(tc.tile_pool(name="lists", bufs=1))
+        keep = ctx.enter_context(tc.tile_pool(name="keep", bufs=1))
+        psum = ctx.enter_context(tc.psum_pool(name="psum", bufs=1))
+
+        def load_list(src, name):
+            tile = lists.tile(list(src.shape), U16, name=name)
+            nc.sync.dma_start(tile[:], src)
+            return tile
+
+        def load_column(src, name):
+            tile = keep.tile([P, PACK], F32, name=name)
+            nc.gpsimd.dma_start(out=tile[:], in_=src.rearrange("(p t) o -> p (t o)", t=PACK))
+            return tile
+
+        def load_rows(src, t, name):
+            tile = keep.tile([P, src.shape[1]], F32, name=name)
+            nc.sync.dma_start(out=tile[:], in_=src.rearrange("(p t) c -> p t c", t=PACK)[:, t, :])
+            return tile
+
+        l2 = load_list(offs2, "l2")
+        ua_rows = [load_rows(ua, 0, "ua0")]
+        l1 = load_list(offs, "l1")
+        ua_rows.append(load_rows(ua, 1, "ua1"))
+        l6 = load_list(offs6, "l6")
+        ua_rows.append(load_rows(ua, 2, "ua2"))
+        l7 = load_list(offs7, "l7")
+        ua_rows.append(load_rows(ua, 3, "ua3"))
+        xw = keep.tile([P, T], I32, name="xw")
+        nc.sync.dma_start(out=xw[:], in_=xt_words[0].rearrange("p c r -> p (c r)").bitcast(I32))
+        va_rows = [load_rows(va, 0, "va0")]
+        l3 = load_list(offs3, "l3")
+        vb_rows = [load_rows(vb, 0, "vb0")]
+        l4 = load_list(offs4, "l4")
+        va_rows.append(load_rows(va, 1, "va1"))
+        l5 = load_list(offs5, "l5")
+        vb_rows.append(load_rows(vb, 1, "vb1"))
+        for t in (2, 3):
+            va_rows.append(load_rows(va, t, f"va{t}"))
+            vb_rows.append(load_rows(vb, t, f"vb{t}"))
+
+        ha_sb = load_column(ha, "ha_sb")
+        xs_stage = keep.tile([4, 4, T // 4], I32, name="xs_stage")
+        nc.gpsimd.dma_start(out=xs_stage[:], in_=xt_scales[0].bitcast(I32).rearrange("(q i) c -> i q c", i=4))
+        ea_sb = load_column(ea, "ea_sb")
+        eb_sb = load_column(eb, "eb_sb")
+        sa_sb = load_column(sa, "sa_sb")
+        sb_sb = load_column(sb, "sb_sb")
+
+        xs = keep.tile([P, T], U8, name="xs")
+        nc.vector.memset(xs[:].bitcast(I32), 0)
+        for q in range(4):
+            nc.vector.tensor_copy(out=xs[32 * q : 32 * q + 4, :].bitcast(I32), in_=xs_stage[:, q, :])
+        xs_picked = keep.tile([P, J], U8, name="xs_picked", align_bytes=64)
+        nc.vector.tensor_copy(xs_picked[:], xs[:].indirect(l1[:]))
+
+        boards = [keep.tile([P, C], F32, name=f"board{t}") for t in range(PACK)]
+        for t in range(PACK):
+            nc.vector.memset(boards[t][:], 0.0)
+
+        wc_rows = [keep.tile([P, R], BF16, name=f"wc_rows{j}") for j in range(PACK)]
+        wc_woven = [keep.tile([P, P * PACK], BF16, name=f"wc_woven{t}", align_bytes=64) for t in range(PACK)]
+        wc_codes = [keep.tile([P, P], U32, name=f"wc_codes{t}", align_bytes=64) for t in range(PACK)]
+        wc_scales = [keep.tile([P, P], U8, name=f"wc_scales{t}", align_bytes=64) for t in range(PACK)]
+
+        def weave_wc(j, t):
+            nc.vector.tensor_copy(
+                out=wc_woven[t][:].rearrange("p (m j) -> p m j", j=PACK)[:, :, j],
+                in_=wc_rows[j][:].rearrange("p (m t) -> p m t", t=PACK)[:, :, t],
+            )
+
+        def quantise_wc(t):
+            nc.vector.quantize_mx(out=wc_codes[t][:].bitcast(FP8X4), scales=wc_scales[t][:], in_=wc_woven[t][:])
+
+        for j in range(PACK):
+            nc.scalar.activation(
+                out=wc_rows[j][:], in_=ua_rows[j][:].indirect(l2[:]), func=ACT.Copy, scale=ha_sb[:, j : j + 1]
+            )
+            if j < PACK - 1:
+                for t in range(PACK):
+                    weave_wc(j, t)
+
+        xw_picked = keep.tile([P, J], U32, name="xw_picked", align_bytes=64)
+        nc.vector.tensor_copy(xw_picked[:], xw[:].bitcast(U32).indirect(l1[:]))
+
+        a_psum = [psum.tile([P, J], F32, name=f"a_psum{t}") for t in range(PACK)]
+        a_sb = [keep.tile([P, J], F32, name=f"a_sb{t}") for t in range(PACK)]
+
+        def first_product(t):
+            nc.tensor.matmul_mx(
+                out=a_psum[t][:],
+                lhsT=wc_codes[t][:].bitcast(FP8X4),
+                lhsT_scale=wc_scales[t][:],
+                rhs=xw_picked[:].bitcast(FP8X4),
+                rhs_scale=xs_picked[:],
+                start=True,
+                stop=True,
+            )
+
+        weave_wc(3, 0)
+        for t in range(PACK):
+            if t + 1 < PACK:
+                weave_wc(3, t + 1)
+            quantise_wc(t)
+            first_product(t)
+
+        base = keep.tile([P, PACK, N], F32, name="base")
+        detail = keep.tile([P, PACK, N], F32, name="detail")
+        for t in range(PACK):
+            nc.scalar.activation(
+                out=base[:, t, :], in_=va_rows[t][:].indirect(l6[:]), func=ACT.Copy, scale=ea_sb[:, t : t + 1]
+            )
+            nc.scalar.activation(
+                out=detail[:, t, :], in_=vb_rows[t][:].indirect(l7[:]), func=ACT.Copy, scale=eb_sb[:, t : t + 1]
+            )
+
+        first = [keep.tile([P, O], F32, name=f"first{t}") for t in range(PACK)]
+        second = [keep.tile([P, O], F32, name=f"second{t}") for t in range(PACK)]
+        diff = keep.tile([P, PACK, O], F32, name="diff")
+
+        def read_board(t):
+            nc.scalar.activation(
+                out=first[t][:], in_=boards[t][:].indirect(l4[:]), func=ACT.Copy, scale=sa_sb[:, t : t + 1]
+            )
+            nc.scalar.activation(
+                out=second[t][:], in_=boards[t][:].indirect(l5[:]), func=ACT.Copy, scale=sb_sb[:, t : t + 1]
+            )
+
+        nc.vector.tensor_copy(out=a_sb[0][:], in_=a_psum[0][:])
+        nc.vector.tensor_copy(boards[0][:].indirect(l3[:]), a_sb[0][:])
+        nc.vector.tensor_copy(out=a_sb[1][:], in_=a_psum[1][:])
+        nc.vector.tensor_copy(out=a_sb[3][:], in_=a_psum[3][:])
+        nc.vector.tensor_copy(boards[1][:].indirect(l3[:]), a_sb[1][:])
+        nc.scalar.activation(out=boards[3][:].indirect(l3[:]), in_=a_sb[3][:], func=ACT.Copy)
+        nc.vector.tensor_copy(out=a_sb[2][:], in_=a_psum[2][:])
+        nc.vector.tensor_copy(boards[2][:].indirect(l3[:]), a_sb[2][:])
+        for t in (0, 3, 1, 2):
+            read_board(t)
+
+        vc_woven = keep.tile([P, N * PACK], BF16, name="vc_woven", align_bytes=64)
+        nc.vector.tensor_tensor(
+            out=vc_woven[:].rearrange("p (c i t) -> p c t i", i=4, t=PACK),
+            in0=base[:].rearrange("p t (c i) -> p c t i", i=4),
+            in1=detail[:].rearrange("p t (c i) -> p c t i", i=4),
+            op=ALU.add,
+        )
+        for t in (0, 3):
+            nc.vector.tensor_tensor(out=diff[:, t, :], in0=first[t][:], in1=second[t][:], op=ALU.subtract)
+        vc_codes = keep.tile([P, N], U32, name="vc_codes", align_bytes=64)
+        vc_scales = keep.tile([P, N], U8, name="vc_scales", align_bytes=64)
+        nc.vector.quantize_mx(out=vc_codes[:].bitcast(FP8X4), scales=vc_scales[:], in_=vc_woven[:])
+        for t in (1, 2):
+            nc.vector.tensor_tensor(out=diff[:, t, :], in0=first[t][:], in1=second[t][:], op=ALU.subtract)
+
+        hid_woven = keep.tile([P, O * PACK], BF16, name="hid_woven", align_bytes=64)
+        nc.scalar.activation(
+            out=hid_woven[:].rearrange("p (c i t) -> p c t i", i=4, t=PACK),
+            in_=diff[:].rearrange("p t (c i) -> p c t i", i=4),
+            func=ACT.Abs,
+        )
+        hid_codes = keep.tile([P, O], U32, name="hid_codes", align_bytes=64)
+        hid_scales = keep.tile([P, O], U8, name="hid_scales", align_bytes=64)
+        nc.vector.quantize_mx(out=hid_codes[:].bitcast(FP8X4), scales=hid_scales[:], in_=hid_woven[:])
+
+        for u in range(N // P):
+            y_psum = psum.tile([P, O], F32, name=f"y_psum{u}")
+            cols = slice(u * P, (u + 1) * P)
+            nc.tensor.matmul_mx(
+                out=y_psum[:],
+                lhsT=vc_codes[:, cols].bitcast(FP8X4),
+                lhsT_scale=vc_scales[:, cols],
+                rhs=hid_codes[:].bitcast(FP8X4),
+                rhs_scale=hid_scales[:],
+                start=True,
+                stop=True,
+            )
+            y_sb = keep.tile([P, O], F32, name=f"y_sb{u}")
+            if u == 0:
+                nc.scalar.copy(out=y_sb[:], in_=y_psum[:])
+                nc.scalar.dma_start(out=out[cols, :], in_=y_sb[:])
+            else:
+                nc.vector.tensor_copy(out=y_sb[:], in_=y_psum[:])
+                nc.sync.dma_start(out=out[cols, :], in_=y_sb[:])

@@ -35,41 +35,37 @@ def tile_picked_tokens_codes_one_boardmixed_basedetail_plain_kernel(
 
         def load_column(src, name):
             tile = keep.tile([P, PACK], F32, name=name)
-            nc.gpsimd.dma_start(out=tile[:], in_=src.rearrange("(p t) o -> p (t o)", t=PACK))
+            nc.sync.dma_start(out=tile[:], in_=src.rearrange("(p t) o -> p (t o)", t=PACK))
             return tile
 
         def load_rows(src, t, name):
-            tile = keep.tile([P, src.shape[1]], F32, name=name)
+            tile = keep.tile([P, src.shape[1]], F32, name=name, tag=name)
             nc.sync.dma_start(out=tile[:], in_=src.rearrange("(p t) c -> p t c", t=PACK)[:, t, :])
             return tile
 
-        l2 = load_list(offs2, "l2")
         ua_rows = [load_rows(ua, 0, "ua0")]
+        l2 = load_list(offs2, "l2")
+        ha_sb = load_column(ha, "ha_sb")
         l1 = load_list(offs, "l1")
-        ua_rows.append(load_rows(ua, 1, "ua1"))
-        l6 = load_list(offs6, "l6")
-        ua_rows.append(load_rows(ua, 2, "ua2"))
-        l7 = load_list(offs7, "l7")
-        ua_rows.append(load_rows(ua, 3, "ua3"))
+        xs_stage = keep.tile([4, 4, T // 4], I32, name="xs_stage")
+        nc.sync.dma_start(out=xs_stage[:], in_=xt_scales[0].bitcast(I32).rearrange("(q i) c -> i q c", i=4))
+        for t in range(1, PACK):
+            ua_rows.append(load_rows(ua, t, f"ua{t}"))
         xw = keep.tile([P, T], I32, name="xw")
         nc.sync.dma_start(out=xw[:], in_=xt_words[0].rearrange("p c r -> p (c r)").bitcast(I32))
+        l6 = load_list(offs6, "l6")
+        ea_sb = load_column(ea, "ea_sb")
         va_rows = [load_rows(va, 0, "va0")]
-        l3 = load_list(offs3, "l3")
+        l7 = load_list(offs7, "l7")
+        eb_sb = load_column(eb, "eb_sb")
         vb_rows = [load_rows(vb, 0, "vb0")]
-        l4 = load_list(offs4, "l4")
-        va_rows.append(load_rows(va, 1, "va1"))
-        l5 = load_list(offs5, "l5")
-        vb_rows.append(load_rows(vb, 1, "vb1"))
-        for t in (2, 3):
+        l3 = load_list(offs3, "l3")
+        for t in range(1, PACK):
             va_rows.append(load_rows(va, t, f"va{t}"))
             vb_rows.append(load_rows(vb, t, f"vb{t}"))
-
-        ha_sb = load_column(ha, "ha_sb")
-        xs_stage = keep.tile([4, 4, T // 4], I32, name="xs_stage")
-        nc.gpsimd.dma_start(out=xs_stage[:], in_=xt_scales[0].bitcast(I32).rearrange("(q i) c -> i q c", i=4))
-        ea_sb = load_column(ea, "ea_sb")
-        eb_sb = load_column(eb, "eb_sb")
+        l4 = load_list(offs4, "l4")
         sa_sb = load_column(sa, "sa_sb")
+        l5 = load_list(offs5, "l5")
         sb_sb = load_column(sb, "sb_sb")
 
         xs = keep.tile([P, T], U8, name="xs")
@@ -83,7 +79,7 @@ def tile_picked_tokens_codes_one_boardmixed_basedetail_plain_kernel(
         for t in range(PACK):
             nc.vector.memset(boards[t][:], 0.0)
 
-        wc_rows = [keep.tile([P, R], BF16, name=f"wc_rows{j}") for j in range(PACK)]
+        wc_rows = [keep.tile([P, R], BF16, name=f"wc_rows{j}", tag=f"wc_rows{j}", align_bytes=64) for j in range(PACK)]
         wc_woven = [keep.tile([P, P * PACK], BF16, name=f"wc_woven{t}", align_bytes=64) for t in range(PACK)]
         wc_codes = [keep.tile([P, P], U32, name=f"wc_codes{t}", align_bytes=64) for t in range(PACK)]
         wc_scales = [keep.tile([P, P], U8, name=f"wc_scales{t}", align_bytes=64) for t in range(PACK)]
@@ -105,11 +101,11 @@ def tile_picked_tokens_codes_one_boardmixed_basedetail_plain_kernel(
                 for t in range(PACK):
                     weave_wc(j, t)
 
-        xw_picked = keep.tile([P, J], U32, name="xw_picked", align_bytes=64)
+        xw_picked = keep.tile([P, J], U32, name="xw_picked", tag="wc_rows2", align_bytes=64)
         nc.vector.tensor_copy(xw_picked[:], xw[:].bitcast(U32).indirect(l1[:]))
 
         a_psum = [psum.tile([P, J], F32, name=f"a_psum{t}") for t in range(PACK)]
-        a_sb = [keep.tile([P, J], F32, name=f"a_sb{t}") for t in range(PACK)]
+        a_sb = [keep.tile([P, J], F32, name=f"a_sb{t}", tag=f"a_sb{t}", align_bytes=64) for t in range(PACK)]
 
         def first_product(t):
             nc.tensor.matmul_mx(
@@ -129,9 +125,11 @@ def tile_picked_tokens_codes_one_boardmixed_basedetail_plain_kernel(
             quantise_wc(t)
             first_product(t)
 
-        base = keep.tile([P, PACK, N], F32, name="base")
-        detail = keep.tile([P, PACK, N], F32, name="detail")
-        for t in range(PACK):
+        parts = keep.tile([P, 2, PACK, N], F32, name="parts", tag="ua3")
+        base = parts[:, 0]
+        detail = parts[:, 1]
+
+        def fetch_parts(t):
             nc.scalar.activation(
                 out=base[:, t, :], in_=va_rows[t][:].indirect(l6[:]), func=ACT.Copy, scale=ea_sb[:, t : t + 1]
             )
@@ -141,7 +139,7 @@ def tile_picked_tokens_codes_one_boardmixed_basedetail_plain_kernel(
 
         first = [keep.tile([P, O], F32, name=f"first{t}") for t in range(PACK)]
         second = [keep.tile([P, O], F32, name=f"second{t}") for t in range(PACK)]
-        diff = keep.tile([P, PACK, O], F32, name="diff")
+        diff = [keep.tile([P, 2, O], F32, name=f"diff{h}") for h in range(2)]
 
         def read_board(t):
             nc.scalar.activation(
@@ -151,38 +149,45 @@ def tile_picked_tokens_codes_one_boardmixed_basedetail_plain_kernel(
                 out=second[t][:], in_=boards[t][:].indirect(l5[:]), func=ACT.Copy, scale=sb_sb[:, t : t + 1]
             )
 
+        def subtract(t):
+            nc.vector.tensor_tensor(out=diff[t // 2][:, t % 2, :], in0=first[t][:], in1=second[t][:], op=ALU.subtract)
+
+        for t in range(3):
+            fetch_parts(t)
         nc.vector.tensor_copy(out=a_sb[0][:], in_=a_psum[0][:])
         nc.vector.tensor_copy(boards[0][:].indirect(l3[:]), a_sb[0][:])
         nc.vector.tensor_copy(out=a_sb[1][:], in_=a_psum[1][:])
         nc.vector.tensor_copy(out=a_sb[3][:], in_=a_psum[3][:])
         nc.vector.tensor_copy(boards[1][:].indirect(l3[:]), a_sb[1][:])
-        nc.scalar.activation(out=boards[3][:].indirect(l3[:]), in_=a_sb[3][:], func=ACT.Copy)
         nc.vector.tensor_copy(out=a_sb[2][:], in_=a_psum[2][:])
         nc.vector.tensor_copy(boards[2][:].indirect(l3[:]), a_sb[2][:])
-        for t in (0, 3, 1, 2):
+        read_board(0)
+        fetch_parts(3)
+        nc.scalar.activation(out=boards[3][:].indirect(l3[:]), in_=a_sb[3][:], func=ACT.Copy)
+        for t in (1, 3, 2):
             read_board(t)
 
         vc_woven = keep.tile([P, N * PACK], BF16, name="vc_woven", align_bytes=64)
-        nc.vector.tensor_tensor(
+        nc.gpsimd.tensor_tensor(
             out=vc_woven[:].rearrange("p (c i t) -> p c t i", i=4, t=PACK),
-            in0=base[:].rearrange("p t (c i) -> p c t i", i=4),
-            in1=detail[:].rearrange("p t (c i) -> p c t i", i=4),
+            in0=base.rearrange("p t (c i) -> p c t i", i=4),
+            in1=detail.rearrange("p t (c i) -> p c t i", i=4),
             op=ALU.add,
         )
-        for t in (0, 3):
-            nc.vector.tensor_tensor(out=diff[:, t, :], in0=first[t][:], in1=second[t][:], op=ALU.subtract)
-        vc_codes = keep.tile([P, N], U32, name="vc_codes", align_bytes=64)
+        vc_codes = keep.tile([P, N], U32, name="vc_codes", tag="a_sb2", align_bytes=64)
         vc_scales = keep.tile([P, N], U8, name="vc_scales", align_bytes=64)
-        nc.vector.quantize_mx(out=vc_codes[:].bitcast(FP8X4), scales=vc_scales[:], in_=vc_woven[:])
-        for t in (1, 2):
-            nc.vector.tensor_tensor(out=diff[:, t, :], in0=first[t][:], in1=second[t][:], op=ALU.subtract)
-
         hid_woven = keep.tile([P, O * PACK], BF16, name="hid_woven", align_bytes=64)
-        nc.scalar.activation(
-            out=hid_woven[:].rearrange("p (c i t) -> p c t i", i=4, t=PACK),
-            in_=diff[:].rearrange("p t (c i) -> p c t i", i=4),
-            func=ACT.Abs,
+        hid_planes = hid_woven[:].rearrange("p (o t) -> p o t", t=PACK)
+        subtract(0)
+        subtract(1)
+        nc.vector.quantize_mx(out=vc_codes[:].bitcast(FP8X4), scales=vc_scales[:], in_=vc_woven[:])
+        early = diff[0][:].rearrange("p t o -> p o t")
+        nc.vector.scalar_tensor_tensor(
+            out=hid_planes[:, :, 0:2], in0=early, scalar=-1.0, in1=early, op0=ALU.mult, op1=ALU.max
         )
+        subtract(3)
+        subtract(2)
+        nc.scalar.activation(out=hid_planes[:, :, 2:4], in_=diff[1][:].rearrange("p t o -> p o t"), func=ACT.Abs)
         hid_codes = keep.tile([P, O], U32, name="hid_codes", align_bytes=64)
         hid_scales = keep.tile([P, O], U8, name="hid_scales", align_bytes=64)
         nc.vector.quantize_mx(out=hid_codes[:].bitcast(FP8X4), scales=hid_scales[:], in_=hid_woven[:])

@@ -39,27 +39,28 @@ def tile_picked_tokens_codes_one_boardmixed_basedetail_plain_kernel(
             return tile
 
         def load_rows(src, t, name):
-            tile = keep.tile([P, src.shape[1]], F32, name=name, tag=name)
+            tile = keep.tile([P, src.shape[1]], F32, name=name, tag=name, align_bytes=64)
             nc.sync.dma_start(out=tile[:], in_=src.rearrange("(p t) c -> p t c", t=PACK)[:, t, :])
             return tile
 
         ua_rows = [load_rows(ua, 0, "ua0")]
         l2 = load_list(offs2, "l2")
         ha_sb = load_column(ha, "ha_sb")
+        ua_rows.append(load_rows(ua, 1, "ua1"))
         l1 = load_list(offs, "l1")
         xs_stage = keep.tile([4, 4, T // 4], I32, name="xs_stage")
         nc.sync.dma_start(out=xs_stage[:], in_=xt_scales[0].bitcast(I32).rearrange("(q i) c -> i q c", i=4))
-        for t in range(1, PACK):
-            ua_rows.append(load_rows(ua, t, f"ua{t}"))
-        xw = keep.tile([P, T], I32, name="xw")
-        nc.sync.dma_start(out=xw[:], in_=xt_words[0].rearrange("p c r -> p (c r)").bitcast(I32))
+        ua_rows.append(load_rows(ua, 2, "ua2"))
         l6 = load_list(offs6, "l6")
         ea_sb = load_column(ea, "ea_sb")
+        l3 = load_list(offs3, "l3")
+        ua_rows.append(load_rows(ua, 3, "ua3"))
+        xw = keep.tile([P, T], I32, name="xw")
+        nc.sync.dma_start(out=xw[:], in_=xt_words[0].rearrange("p c r -> p (c r)").bitcast(I32))
         va_rows = [load_rows(va, 0, "va0")]
         l7 = load_list(offs7, "l7")
         eb_sb = load_column(eb, "eb_sb")
         vb_rows = [load_rows(vb, 0, "vb0")]
-        l3 = load_list(offs3, "l3")
         for t in range(1, PACK):
             va_rows.append(load_rows(va, t, f"va{t}"))
             vb_rows.append(load_rows(vb, t, f"vb{t}"))
@@ -104,12 +105,14 @@ def tile_picked_tokens_codes_one_boardmixed_basedetail_plain_kernel(
         xw_picked = keep.tile([P, J], U32, name="xw_picked", tag="wc_rows2", align_bytes=64)
         nc.vector.tensor_copy(xw_picked[:], xw[:].bitcast(U32).indirect(l1[:]))
 
-        a_psum = [psum.tile([P, J], F32, name=f"a_psum{t}") for t in range(PACK)]
-        a_sb = [keep.tile([P, J], F32, name=f"a_sb{t}", tag=f"a_sb{t}", align_bytes=64) for t in range(PACK)]
+        a_late_psum = psum.tile([P, 2, J], F32, name="a_late_psum")
+        a_psum = [psum.tile([P, J], F32, name=f"a_psum{t}")[:] for t in range(2)] + [a_late_psum[:, 0], a_late_psum[:, 1]]
+        a_late = keep.tile([P, 2, J], F32, name="a_late", tag="va2", align_bytes=64)
+        a_sb = [keep.tile([P, J], F32, name=f"a_sb{t}")[:] for t in range(2)] + [a_late[:, 0], a_late[:, 1]]
 
         def first_product(t):
             nc.tensor.matmul_mx(
-                out=a_psum[t][:],
+                out=a_psum[t],
                 lhsT=wc_codes[t][:].bitcast(FP8X4),
                 lhsT_scale=wc_scales[t][:],
                 rhs=xw_picked[:].bitcast(FP8X4),
@@ -125,7 +128,7 @@ def tile_picked_tokens_codes_one_boardmixed_basedetail_plain_kernel(
             quantise_wc(t)
             first_product(t)
 
-        parts = keep.tile([P, 2, PACK, N], F32, name="parts", tag="ua3")
+        parts = keep.tile([P, 2, PACK, N], F32, name="parts", tag="ua3", align_bytes=64)
         base = parts[:, 0]
         detail = parts[:, 1]
 
@@ -137,56 +140,54 @@ def tile_picked_tokens_codes_one_boardmixed_basedetail_plain_kernel(
                 out=detail[:, t, :], in_=vb_rows[t][:].indirect(l7[:]), func=ACT.Copy, scale=eb_sb[:, t : t + 1]
             )
 
-        first = [keep.tile([P, O], F32, name=f"first{t}") for t in range(PACK)]
-        second = [keep.tile([P, O], F32, name=f"second{t}") for t in range(PACK)]
         diff = [keep.tile([P, 2, O], F32, name=f"diff{h}") for h in range(2)]
 
         def read_board(t):
             nc.scalar.activation(
-                out=first[t][:], in_=boards[t][:].indirect(l4[:]), func=ACT.Copy, scale=sa_sb[:, t : t + 1]
+                out=first[t], in_=boards[t][:].indirect(l4[:]), func=ACT.Copy, scale=sa_sb[:, t : t + 1]
             )
             nc.scalar.activation(
-                out=second[t][:], in_=boards[t][:].indirect(l5[:]), func=ACT.Copy, scale=sb_sb[:, t : t + 1]
+                out=second[t], in_=boards[t][:].indirect(l5[:]), func=ACT.Copy, scale=sb_sb[:, t : t + 1]
             )
 
         def subtract(t):
-            nc.vector.tensor_tensor(out=diff[t // 2][:, t % 2, :], in0=first[t][:], in1=second[t][:], op=ALU.subtract)
+            nc.vector.tensor_tensor(out=diff[t // 2][:, t % 2, :], in0=first[t], in1=second[t], op=ALU.subtract)
 
-        for t in range(3):
+        for t in range(2):
             fetch_parts(t)
-        nc.vector.tensor_copy(out=a_sb[0][:], in_=a_psum[0][:])
-        nc.vector.tensor_copy(boards[0][:].indirect(l3[:]), a_sb[0][:])
-        nc.vector.tensor_copy(out=a_sb[1][:], in_=a_psum[1][:])
-        nc.vector.tensor_copy(out=a_sb[3][:], in_=a_psum[3][:])
-        nc.vector.tensor_copy(boards[1][:].indirect(l3[:]), a_sb[1][:])
-        nc.vector.tensor_copy(out=a_sb[2][:], in_=a_psum[2][:])
-        nc.vector.tensor_copy(boards[2][:].indirect(l3[:]), a_sb[2][:])
-        read_board(0)
+            nc.vector.tensor_copy(out=a_sb[t], in_=a_psum[t])
+            nc.vector.tensor_copy(boards[t][:].indirect(l3[:]), a_sb[t])
+        fetch_parts(2)
+        nc.scalar.copy(out=a_late[:], in_=a_late_psum[:])
+        nc.vector.tensor_copy(boards[2][:].indirect(l3[:]), a_sb[2])
         fetch_parts(3)
-        nc.scalar.activation(out=boards[3][:].indirect(l3[:]), in_=a_sb[3][:], func=ACT.Copy)
-        for t in (1, 3, 2):
+        nc.scalar.activation(out=boards[3][:].indirect(l3[:]), in_=a_sb[3], func=ACT.Copy)
+        picked = keep.tile([P, PACK, 2, O], F32, name="picked", tag="vb3", align_bytes=64)
+        first = [picked[:, t, 0] for t in range(PACK)]
+        second = [picked[:, t, 1] for t in range(PACK)]
+        for t in (0, 1, 3, 2):
             read_board(t)
 
-        vc_woven = keep.tile([P, N * PACK], BF16, name="vc_woven", align_bytes=64)
-        nc.gpsimd.tensor_tensor(
+        vc_woven = keep.tile([P, N * PACK], BF16, name="vc_woven", tag="va2", align_bytes=64)
+        nc.vector.tensor_tensor(
             out=vc_woven[:].rearrange("p (c i t) -> p c t i", i=4, t=PACK),
             in0=base.rearrange("p t (c i) -> p c t i", i=4),
             in1=detail.rearrange("p t (c i) -> p c t i", i=4),
             op=ALU.add,
         )
-        vc_codes = keep.tile([P, N], U32, name="vc_codes", tag="a_sb2", align_bytes=64)
+        vc_codes = keep.tile([P, N], U32, name="vc_codes", align_bytes=64)
         vc_scales = keep.tile([P, N], U8, name="vc_scales", align_bytes=64)
         hid_woven = keep.tile([P, O * PACK], BF16, name="hid_woven", align_bytes=64)
         hid_planes = hid_woven[:].rearrange("p (o t) -> p o t", t=PACK)
         subtract(0)
         subtract(1)
         nc.vector.quantize_mx(out=vc_codes[:].bitcast(FP8X4), scales=vc_scales[:], in_=vc_woven[:])
+        subtract(3)
+        subtract(2)
         early = diff[0][:].rearrange("p t o -> p o t")
         nc.vector.scalar_tensor_tensor(
             out=hid_planes[:, :, 0:2], in0=early, scalar=-1.0, in1=early, op0=ALU.mult, op1=ALU.max
         )
-        subtract(3)
-        subtract(2)
         nc.scalar.activation(out=hid_planes[:, :, 2:4], in_=diff[1][:].rearrange("p t o -> p o t"), func=ACT.Abs)
         hid_codes = keep.tile([P, O], U32, name="hid_codes", align_bytes=64)
         hid_scales = keep.tile([P, O], U8, name="hid_scales", align_bytes=64)

@@ -26,6 +26,7 @@ def tile_picked_tokens_codes_one_boardmixed_basedetail_plain_kernel(
     with ExitStack() as ctx:
         lists = ctx.enter_context(tc.tile_pool(name="lists", bufs=1))
         keep = ctx.enter_context(tc.tile_pool(name="keep", bufs=1))
+        reuse = ctx.enter_context(tc.tile_pool(name="reuse", bufs=1))
         psum = ctx.enter_context(tc.psum_pool(name="psum", bufs=1))
 
         def load_list(src, name):
@@ -39,7 +40,10 @@ def tile_picked_tokens_codes_one_boardmixed_basedetail_plain_kernel(
             return tile
 
         def load_rows(src, t, name):
-            tile = keep.tile([P, src.shape[1]], F32, name=name, tag=name, align_bytes=64)
+            if name == "vb3":
+                tile = reuse.tile([P, src.shape[1]], F32, name=name, offset=1024)
+            else:
+                tile = keep.tile([P, src.shape[1]], F32, name=name, tag=name, align_bytes=64)
             nc.sync.dma_start(out=tile[:], in_=src.rearrange("(p t) c -> p t c", t=PACK)[:, t, :])
             return tile
 
@@ -61,12 +65,15 @@ def tile_picked_tokens_codes_one_boardmixed_basedetail_plain_kernel(
         l7 = load_list(offs7, "l7")
         eb_sb = load_column(eb, "eb_sb")
         vb_rows = [load_rows(vb, 0, "vb0")]
-        for t in range(1, PACK):
-            va_rows.append(load_rows(va, t, f"va{t}"))
-            vb_rows.append(load_rows(vb, t, f"vb{t}"))
+        va_rows.append(load_rows(va, 1, "va1"))
+        vb_rows.append(load_rows(vb, 1, "vb1"))
+        va_rows.append(load_rows(va, 2, "va2"))
         l4 = load_list(offs4, "l4")
+        vb_rows.append(load_rows(vb, 2, "vb2"))
         sa_sb = load_column(sa, "sa_sb")
         l5 = load_list(offs5, "l5")
+        va_rows.append(load_rows(va, 3, "va3"))
+        vb_rows.append(load_rows(vb, 3, "vb3"))
         sb_sb = load_column(sb, "sb_sb")
 
         xs = keep.tile([P, T], U8, name="xs")
@@ -107,7 +114,7 @@ def tile_picked_tokens_codes_one_boardmixed_basedetail_plain_kernel(
 
         a_late_psum = psum.tile([P, 2, J], F32, name="a_late_psum")
         a_psum = [psum.tile([P, J], F32, name=f"a_psum{t}")[:] for t in range(2)] + [a_late_psum[:, 0], a_late_psum[:, 1]]
-        a_late = keep.tile([P, 2, J], F32, name="a_late", tag="va2", align_bytes=64)
+        a_late = reuse.tile([P, 2, J], F32, name="a_late", offset=0)
         a_sb = [keep.tile([P, J], F32, name=f"a_sb{t}")[:] for t in range(2)] + [a_late[:, 0], a_late[:, 1]]
 
         def first_product(t):
@@ -140,7 +147,7 @@ def tile_picked_tokens_codes_one_boardmixed_basedetail_plain_kernel(
                 out=detail[:, t, :], in_=vb_rows[t][:].indirect(l7[:]), func=ACT.Copy, scale=eb_sb[:, t : t + 1]
             )
 
-        diff = [keep.tile([P, 2, O], F32, name=f"diff{h}") for h in range(2)]
+        diff = [reuse.tile([P, 2, O], F32, name="diff0", offset=0), keep.tile([P, 2, O], F32, name="diff1")]
 
         def read_board(t):
             nc.scalar.activation(
@@ -153,37 +160,44 @@ def tile_picked_tokens_codes_one_boardmixed_basedetail_plain_kernel(
         def subtract(t):
             nc.vector.tensor_tensor(out=diff[t // 2][:, t % 2, :], in0=first[t], in1=second[t], op=ALU.subtract)
 
-        for t in range(2):
+        vc_woven = keep.tile([P, N * PACK], BF16, name="vc_woven", align_bytes=64)
+        vc_planes = vc_woven[:].rearrange("p (n t) -> p n t", t=PACK)
+
+        def add_parts(h):
+            pair = slice(2 * h, 2 * h + 2)
+            nc.gpsimd.tensor_tensor(
+                out=vc_planes[:, :, pair],
+                in0=base[:, pair, :].rearrange("p t n -> p n t"),
+                in1=detail[:, pair, :].rearrange("p t n -> p n t"),
+                op=ALU.add,
+            )
+
+        for t in range(PACK):
             fetch_parts(t)
+            if t % 2 == 1:
+                add_parts(t // 2)
+        for t in range(2):
             nc.vector.tensor_copy(out=a_sb[t], in_=a_psum[t])
+        for t in range(2):
             nc.vector.tensor_copy(boards[t][:].indirect(l3[:]), a_sb[t])
-        fetch_parts(2)
-        nc.scalar.copy(out=a_late[:], in_=a_late_psum[:])
-        nc.vector.tensor_copy(boards[2][:].indirect(l3[:]), a_sb[2])
-        fetch_parts(3)
-        nc.scalar.activation(out=boards[3][:].indirect(l3[:]), in_=a_sb[3], func=ACT.Copy)
-        picked = keep.tile([P, PACK, 2, O], F32, name="picked", tag="vb3", align_bytes=64)
+        nc.vector.tensor_copy(out=a_late[:], in_=a_late_psum[:])
+        nc.vector.tensor_copy(boards[3][:].indirect(l3[:]), a_sb[3])
+        picked = reuse.tile([P, PACK, 2, O], F32, name="picked", offset=2048)
         first = [picked[:, t, 0] for t in range(PACK)]
         second = [picked[:, t, 1] for t in range(PACK)]
-        for t in (0, 1, 3, 2):
+        for t in range(2):
+            read_board(t)
+        nc.scalar.activation(out=boards[2][:].indirect(l3[:]), in_=a_sb[2], func=ACT.Copy)
+        for t in range(2, PACK):
             read_board(t)
 
-        vc_woven = keep.tile([P, N * PACK], BF16, name="vc_woven", tag="va2", align_bytes=64)
-        nc.vector.tensor_tensor(
-            out=vc_woven[:].rearrange("p (c i t) -> p c t i", i=4, t=PACK),
-            in0=base.rearrange("p t (c i) -> p c t i", i=4),
-            in1=detail.rearrange("p t (c i) -> p c t i", i=4),
-            op=ALU.add,
-        )
-        vc_codes = keep.tile([P, N], U32, name="vc_codes", align_bytes=64)
+        vc_codes = reuse.tile([P, N], U32, name="vc_codes", offset=1024, align_bytes=64)
         vc_scales = keep.tile([P, N], U8, name="vc_scales", align_bytes=64)
         hid_woven = keep.tile([P, O * PACK], BF16, name="hid_woven", align_bytes=64)
         hid_planes = hid_woven[:].rearrange("p (o t) -> p o t", t=PACK)
-        subtract(0)
-        subtract(1)
         nc.vector.quantize_mx(out=vc_codes[:].bitcast(FP8X4), scales=vc_scales[:], in_=vc_woven[:])
-        subtract(3)
-        subtract(2)
+        for t in range(PACK):
+            subtract(t)
         early = diff[0][:].rearrange("p t o -> p o t")
         nc.vector.scalar_tensor_tensor(
             out=hid_planes[:, :, 0:2], in0=early, scalar=-1.0, in1=early, op0=ALU.mult, op1=ALU.max

@@ -34,9 +34,9 @@ def tile_picked_tokens_codes_one_boardmixed_basedetail_plain_kernel(
             nc.sync.dma_start(tile[:], src)
             return tile
 
-        def load_column(src, name):
+        def load_column(queue, src, name):
             tile = keep.tile([P, PACK], F32, name=name)
-            nc.sync.dma_start(out=tile[:], in_=src.rearrange("(p t) o -> p (t o)", t=PACK))
+            queue.dma_start(out=tile[:], in_=src.rearrange("(p t) o -> p (t o)", t=PACK))
             return tile
 
         def load_rows(src, t, name):
@@ -49,32 +49,29 @@ def tile_picked_tokens_codes_one_boardmixed_basedetail_plain_kernel(
 
         ua_rows = [load_rows(ua, 0, "ua0")]
         l2 = load_list(offs2, "l2")
-        ha_sb = load_column(ha, "ha_sb")
+        ha_sb = load_column(nc.sync, ha, "ha_sb")
         ua_rows.append(load_rows(ua, 1, "ua1"))
         l1 = load_list(offs, "l1")
         xs_stage = keep.tile([4, 4, T // 4], I32, name="xs_stage")
         nc.sync.dma_start(out=xs_stage[:], in_=xt_scales[0].bitcast(I32).rearrange("(q i) c -> i q c", i=4))
         ua_rows.append(load_rows(ua, 2, "ua2"))
         l6 = load_list(offs6, "l6")
-        ea_sb = load_column(ea, "ea_sb")
         l3 = load_list(offs3, "l3")
+        l4 = load_list(offs4, "l4")
         ua_rows.append(load_rows(ua, 3, "ua3"))
         xw = keep.tile([P, T], I32, name="xw")
         nc.sync.dma_start(out=xw[:], in_=xt_words[0].rearrange("p c r -> p (c r)").bitcast(I32))
         va_rows = [load_rows(va, 0, "va0")]
         l7 = load_list(offs7, "l7")
-        eb_sb = load_column(eb, "eb_sb")
-        vb_rows = [load_rows(vb, 0, "vb0")]
-        va_rows.append(load_rows(va, 1, "va1"))
-        vb_rows.append(load_rows(vb, 1, "vb1"))
-        va_rows.append(load_rows(va, 2, "va2"))
-        l4 = load_list(offs4, "l4")
-        vb_rows.append(load_rows(vb, 2, "vb2"))
-        sa_sb = load_column(sa, "sa_sb")
         l5 = load_list(offs5, "l5")
-        va_rows.append(load_rows(va, 3, "va3"))
-        vb_rows.append(load_rows(vb, 3, "vb3"))
-        sb_sb = load_column(sb, "sb_sb")
+        vb_rows = [load_rows(vb, 0, "vb0")]
+        for t in range(1, PACK):
+            va_rows.append(load_rows(va, t, f"va{t}"))
+            vb_rows.append(load_rows(vb, t, f"vb{t}"))
+        ea_sb = load_column(nc.gpsimd, ea, "ea_sb")
+        eb_sb = load_column(nc.gpsimd, eb, "eb_sb")
+        sa_sb = load_column(nc.gpsimd, sa, "sa_sb")
+        sb_sb = load_column(nc.gpsimd, sb, "sb_sb")
 
         xs = keep.tile([P, T], U8, name="xs")
         nc.vector.memset(xs[:].bitcast(I32), 0)

from contextlib import ExitStack

import concourse.mybir as mybir

K, J, R, T, F, C, O, N, S, Z = 512, 256, 512, 512, 2048, 512, 128, 256, 512, 512
FLOPS = 2 * K * R * J + 2 * R * N * O

F32 = mybir.dt.float32
BF16 = mybir.dt.bfloat16
I32 = mybir.dt.int32
U32 = mybir.dt.uint32
U16 = mybir.dt.uint16
U8 = mybir.dt.uint8
FP8X4 = mybir.dt.float8_e4m3fn_x4
ALU = mybir.AluOpType
ACT = mybir.ActivationFunctionType

P = 128
PACK = 4


def tile_picked_tokens_codes_one_boardmixed_basedetail_plain_kernel(
    tc, xt_words, xt_scales, ua, ha, sa, sb, va, vb, ea, eb, offs, offs2, offs3, offs4, offs5, offs6, offs7, out
):
    nc = tc.nc
    with ExitStack() as ctx:
        lists = ctx.enter_context(tc.tile_pool(name="lists", bufs=1))
        keep = ctx.enter_context(tc.tile_pool(name="keep", bufs=1))
        reuse = ctx.enter_context(tc.tile_pool(name="reuse", bufs=1))
        psum = ctx.enter_context(tc.psum_pool(name="psum", bufs=1))

        def load_list(src, name):
            tile = lists.tile(list(src.shape), U16, name=name)
            nc.sync.dma_start(tile[:], src)
            return tile

        def load_column(queue, src, name):
            tile = keep.tile([P, PACK], F32, name=name)
            queue.dma_start(out=tile[:], in_=src.rearrange("(p t) o -> p (t o)", t=PACK))
            return tile

        def load_rows(src, t, name):
            if name == "vb3":
                tile = reuse.tile([P, src.shape[1]], F32, name=name, offset=1024)
            else:
                tile = keep.tile([P, src.shape[1]], F32, name=name, tag=name, align_bytes=64)
            nc.sync.dma_start(out=tile[:], in_=src.rearrange("(p t) c -> p t c", t=PACK)[:, t, :])
            return tile

        ua_rows = [load_rows(ua, 0, "ua0")]
        l2 = load_list(offs2, "l2")
        ha_sb = load_column(nc.sync, ha, "ha_sb")
        ua_rows.append(load_rows(ua, 1, "ua1"))
        l1 = load_list(offs, "l1")
        xs_stage = keep.tile([4, 4, T // 4], I32, name="xs_stage")
        nc.sync.dma_start(out=xs_stage[:], in_=xt_scales[0].bitcast(I32).rearrange("(q i) c -> i q c", i=4))
        ua_rows.append(load_rows(ua, 2, "ua2"))
        l6 = load_list(offs6, "l6")
        l3 = load_list(offs3, "l3")
        l4 = load_list(offs4, "l4")
        ua_rows.append(load_rows(ua, 3, "ua3"))
        xw = keep.tile([P, T], I32, name="xw")
        nc.sync.dma_start(out=xw[:], in_=xt_words[0].rearrange("p c r -> p (c r)").bitcast(I32))
        va_rows = [load_rows(va, 0, "va0")]
        l7 = load_list(offs7, "l7")
        l5 = load_list(offs5, "l5")
        vb_rows = [load_rows(vb, 0, "vb0")]
        for t in range(1, PACK):
            va_rows.append(load_rows(va, t, f"va{t}"))
            vb_rows.append(load_rows(vb, t, f"vb{t}"))
        ea_sb = load_column(nc.gpsimd, ea, "ea_sb")
        eb_sb = load_column(nc.gpsimd, eb, "eb_sb")
        sa_sb = load_column(nc.gpsimd, sa, "sa_sb")
        sb_sb = load_column(nc.gpsimd, sb, "sb_sb")

        xs = keep.tile([P, T], U8, name="xs")
        nc.vector.memset(xs[:].bitcast(I32), 0)
        for q in range(4):
            nc.vector.tensor_copy(out=xs[32 * q : 32 * q + 4, :].bitcast(I32), in_=xs_stage[:, q, :])
        xs_picked = keep.tile([P, J], U8, name="xs_picked", align_bytes=64)
        nc.vector.tensor_copy(xs_picked[:], xs[:].indirect(l1[:]))

        boards = [keep.tile([P, C], F32, name=f"board{t}") for t in range(PACK)]
        for t in range(PACK):
            nc.vector.memset(boards[t][:], 0.0)

        wc_rows = [keep.tile([P, R], BF16, name=f"wc_rows{j}", tag=f"wc_rows{j}", align_bytes=64) for j in range(PACK)]
        wc_woven = [keep.tile([P, P * PACK], BF16, name=f"wc_woven{t}", align_bytes=64) for t in range(PACK)]
        wc_codes = [keep.tile([P, P], U32, name=f"wc_codes{t}", align_bytes=64) for t in range(PACK)]
        wc_scales = [keep.tile([P, P], U8, name=f"wc_scales{t}", align_bytes=64) for t in range(PACK)]

        def weave_wc(j, t):
            nc.vector.tensor_copy(
                out=wc_woven[t][:].rearrange("p (m j) -> p m j", j=PACK)[:, :, j],
                in_=wc_rows[j][:].rearrange("p (m t) -> p m t", t=PACK)[:, :, t],
            )

        def quantise_wc(t):
            nc.vector.quantize_mx(out=wc_codes[t][:].bitcast(FP8X4), scales=wc_scales[t][:], in_=wc_woven[t][:])

        for j in range(PACK):
            nc.scalar.activation(
                out=wc_rows[j][:], in_=ua_rows[j][:].indirect(l2[:]), func=ACT.Copy, scale=ha_sb[:, j : j + 1]
            )
            if j < PACK - 1:
                for t in range(PACK):
                    weave_wc(j, t)

        xw_picked = keep.tile([P, J], U32, name="xw_picked", tag="wc_rows2", align_bytes=64)
        nc.vector.tensor_copy(xw_picked[:], xw[:].bitcast(U32).indirect(l1[:]))

        a_late_psum = psum.tile([P, 2, J], F32, name="a_late_psum")
        a_psum = [psum.tile([P, J], F32, name=f"a_psum{t}")[:] for t in range(2)] + [a_late_psum[:, 0], a_late_psum[:, 1]]
        a_late = reuse.tile([P, 2, J], F32, name="a_late", offset=0)
        a_sb = [keep.tile([P, J], F32, name=f"a_sb{t}")[:] for t in range(2)] + [a_late[:, 0], a_late[:, 1]]

        def first_product(t):
            nc.tensor.matmul_mx(
                out=a_psum[t],
                lhsT=wc_codes[t][:].bitcast(FP8X4),
                lhsT_scale=wc_scales[t][:],
                rhs=xw_picked[:].bitcast(FP8X4),
                rhs_scale=xs_picked[:],
                start=True,
                stop=True,
            )

        weave_wc(3, 0)
        for t in range(PACK):
            if t + 1 < PACK:
                weave_wc(3, t + 1)
            quantise_wc(t)
            first_product(t)

        parts = keep.tile([P, 2, PACK, N], F32, name="parts", tag="ua3", align_bytes=64)
        base = parts[:, 0]
        detail = parts[:, 1]

        def fetch_parts(t):
            nc.scalar.activation(
                out=base[:, t, :], in_=va_rows[t][:].indirect(l6[:]), func=ACT.Copy, scale=ea_sb[:, t : t + 1]
            )
            nc.scalar.activation(
                out=detail[:, t, :], in_=vb_rows[t][:].indirect(l7[:]), func=ACT.Copy, scale=eb_sb[:, t : t + 1]
            )

        diff = [reuse.tile([P, 2, O], F32, name="diff0", offset=0), keep.tile([P, 2, O], F32, name="diff1")]

        def read_board(t):
            nc.scalar.activation(
                out=first[t], in_=boards[t][:].indirect(l4[:]), func=ACT.Copy, scale=sa_sb[:, t : t + 1]
            )
            nc.scalar.activation(
                out=second[t], in_=boards[t][:].indirect(l5[:]), func=ACT.Copy, scale=sb_sb[:, t : t + 1]
            )

        def subtract(t):
            nc.vector.tensor_tensor(out=diff[t // 2][:, t % 2, :], in0=first[t], in1=second[t], op=ALU.subtract)

        vc_woven = keep.tile([P, N * PACK], BF16, name="vc_woven", align_bytes=64)
        vc_planes = vc_woven[:].rearrange("p (n t) -> p n t", t=PACK)

        def add_parts(h):
            pair = slice(2 * h, 2 * h + 2)
            nc.gpsimd.tensor_tensor(
                out=vc_planes[:, :, pair],
                in0=base[:, pair, :].rearrange("p t n -> p n t"),
                in1=detail[:, pair, :].rearrange("p t n -> p n t"),
                op=ALU.add,
            )

        for t in range(PACK):
            fetch_parts(t)
            if t % 2 == 1:
                add_parts(t // 2)
        for t in range(2):
            nc.vector.tensor_copy(out=a_sb[t], in_=a_psum[t])
        for t in range(2):
            nc.vector.tensor_copy(boards[t][:].indirect(l3[:]), a_sb[t])
        nc.vector.tensor_copy(out=a_late[:], in_=a_late_psum[:])
        nc.vector.tensor_copy(boards[3][:].indirect(l3[:]), a_sb[3])
        picked = reuse.tile([P, PACK, 2, O], F32, name="picked", offset=2048)
        first = [picked[:, t, 0] for t in range(PACK)]
        second = [picked[:, t, 1] for t in range(PACK)]
        for t in range(2):
            read_board(t)
        nc.scalar.activation(out=boards[2][:].indirect(l3[:]), in_=a_sb[2], func=ACT.Copy)
        for t in range(2, PACK):
            read_board(t)

        vc_codes = reuse.tile([P, N], U32, name="vc_codes", offset=1024, align_bytes=64)
        vc_scales = keep.tile([P, N], U8, name="vc_scales", align_bytes=64)
        hid_woven = keep.tile([P, O * PACK], BF16, name="hid_woven", align_bytes=64)
        hid_planes = hid_woven[:].rearrange("p (o t) -> p o t", t=PACK)
        nc.vector.quantize_mx(out=vc_codes[:].bitcast(FP8X4), scales=vc_scales[:], in_=vc_woven[:])
        for t in range(PACK):
            subtract(t)
        early = diff[0][:].rearrange("p t o -> p o t")
        nc.vector.scalar_tensor_tensor(
            out=hid_planes[:, :, 0:2], in0=early, scalar=-1.0, in1=early, op0=ALU.mult, op1=ALU.max
        )
        nc.scalar.activation(out=hid_planes[:, :, 2:4], in_=diff[1][:].rearrange("p t o -> p o t"), func=ACT.Abs)
        hid_codes = keep.tile([P, O], U32, name="hid_codes", align_bytes=64)
        hid_scales = keep.tile([P, O], U8, name="hid_scales", align_bytes=64)
        nc.vector.quantize_mx(out=hid_codes[:].bitcast(FP8X4), scales=hid_scales[:], in_=hid_woven[:])

        for u in range(N // P):
            y_psum = psum.tile([P, O], F32, name=f"y_psum{u}")
            cols = slice(u * P, (u + 1) * P)
            nc.tensor.matmul_mx(
                out=y_psum[:],
                lhsT=vc_codes[:, cols].bitcast(FP8X4),
                lhsT_scale=vc_scales[:, cols],
                rhs=hid_codes[:].bitcast(FP8X4),
                rhs_scale=hid_scales[:],
                start=True,
                stop=True,
            )
            y_sb = keep.tile([P, O], F32, name=f"y_sb{u}")
            if u == 0:
                nc.scalar.copy(out=y_sb[:], in_=y_psum[:])
                nc.scalar.dma_start(out=out[cols, :], in_=y_sb[:])
            else:
                nc.vector.tensor_copy(out=y_sb[:], in_=y_psum[:])
                nc.sync.dma_start(out=out[cols, :], in_=y_sb[:])
